import numpy as np
import ml_dtypes


def mxq(x, axis, fmt="e4m3"):
    dtype, down = {"e4m3": (ml_dtypes.float8_e4m3fn, 7), "e5m2": (ml_dtypes.float8_e5m2, 14)}[fmt]
    v = np.moveaxis(np.asarray(x, np.float32).astype(ml_dtypes.bfloat16).astype(np.float64), axis, -1)
    blocks = v.reshape(v.shape[:-1] + (-1, 32))
    amax = np.abs(blocks).max(-1, keepdims=True)
    byte = np.maximum(np.where(amax > 0, np.frexp(amax)[1] - 1 + 127, 0) - down, 1)
    scale = np.exp2(byte - 127.0)
    codes = (blocks / scale).astype(np.float32).astype(dtype).astype(np.float64)
    return np.moveaxis((codes * scale).reshape(v.shape), -1, axis)


WIDE = False


def mx_kscale(k):
    if not WIDE:
        return np.ones(k)
    levels = np.array([30, -30])
    if k % 512:
        return np.exp2(np.random.permutation(np.resize(levels, k // 32))).repeat(32)
    a = np.empty((k // 512, 16))
    for p in range(k // 512):
        a[p, :8] = np.random.permutation(np.resize(levels, 8))
        for g in range(8):
            far = levels[np.abs(levels - a[p, g]) >= 10]
            a[p, g + 8] = far[np.random.randint(len(far))]
    return np.exp2(a.ravel()).repeat(32)


BF16 = ml_dtypes.bfloat16


def bf(x):
    return np.asarray(x, np.float32).astype(BF16)


def f64(x):
    return np.asarray(x).astype(np.float64)


E2M1 = np.array([0.0, 0.5, 1.0, 1.5, 2.0, 3.0, 4.0, 6.0, -0.0, -0.5, -1.0, -1.5, -2.0, -3.0, -4.0, -6.0])


def pack_weight(w, fmt):
    k, n = w.shape
    w = f64(bf(w)).reshape(k // 32, 32, n)
    amax = np.abs(w).max(1)
    if fmt in ("e4m3", "e5m2"):
        byte = np.frexp(amax)[1] - 1 + 127 - (7 if fmt == "e4m3" else 14)
    else:
        mant, ex = np.frexp(amax / 6.0)
        byte = np.where(mant > 0.5, ex, ex - 1) + 127
    byte = np.clip(np.where(amax > 0, byte, 1), 1, 254)
    scaled = (w * np.exp2(127.0 - byte)[:, None, :]).reshape(k, n).astype(np.float32)
    by_word = np.ascontiguousarray(scaled.reshape(k // 512, 128, 4, n).transpose(0, 1, 3, 2))
    if fmt in ("e4m3", "e5m2"):
        words = by_word.astype(ml_dtypes.float8_e4m3fn if fmt == "e4m3" else ml_dtypes.float8_e5m2).view(np.uint8)
    else:
        c = by_word.astype(ml_dtypes.float4_e2m1fn).view(np.uint8) & 0xF
        words = c[..., 0::2] | (c[..., 1::2] << 4)
    return np.ascontiguousarray(words), np.ascontiguousarray(byte.astype(np.uint8).reshape(k // 512, 16, n))


def unpack_weight(words, scales, fmt):
    g, p, n, _ = words.shape
    if fmt in ("e4m3", "e5m2"):
        vals = np.ascontiguousarray(words).view(ml_dtypes.float8_e4m3fn if fmt == "e4m3" else ml_dtypes.float8_e5m2).astype(np.float64)
    else:
        nib = np.empty((g, p, n, 4), np.uint8)
        nib[..., 0::2] = words & 0xF
        nib[..., 1::2] = words >> 4
        vals = E2M1[nib]
    vals = vals * np.repeat(np.exp2(scales.astype(np.float64) - 127.0), 8, axis=1)[..., None]
    return vals.transpose(0, 1, 3, 2).reshape(g * 512, n)

def planes(Y):
    n, m = Y.shape
    b = f64(bf(Y)).reshape(n // 32, 32, m)
    amax = np.abs(b).max(1)
    byte = np.clip(np.where(amax > 0, np.frexp(amax)[1] - 1 + 127 - 7, 1), 1, 254)
    codes = (b * np.exp2(127.0 - byte)[:, None, :]).reshape(n, m).astype(np.float32).astype(ml_dtypes.float8_e4m3fn).view(np.uint8)
    words = codes.reshape(n // 512, 128, 4, m).transpose(0, 1, 3, 2)
    return np.ascontiguousarray(words), np.ascontiguousarray(byte.astype(np.uint8).reshape(n // 512, 16, m))


T, D, A, K, C = 1536, 32, 32, 1024, 1024


def setup_inputs():
    s = mx_kscale(K)
    r = np.random.randn(T + D - 1, A) * np.exp(0.7 * np.random.randn(T + D - 1, A)) / np.exp(0.49)
    r = f64(bf(r))
    x = np.concatenate([r[D - 1 - d:D - 1 - d + T] for d in range(D)], axis=1)
    taps = np.stack([x[:, 0], x[:, A]], axis=1)
    gain = np.exp(0.8 * np.random.randn(C))
    lin = np.random.randn(K, C) * gain / np.sqrt(K)
    quad0 = 0.8 * np.random.randn(K, C) * gain / np.sqrt(K)
    quad1 = 0.8 * np.random.randn(K, C) * gain / np.sqrt(K)
    kernels = np.concatenate([lin, quad0, quad1], axis=1) / s[:, None]
    x_words, x_scales = pack_weight((x * s).T, "e5m2")
    return {"x_words": x_words, "x_scales": x_scales,
            "taps": bf(taps), "kernels": bf(kernels)}

def reference(x_words, x_scales, taps, kernels):
    V = unpack_weight(x_words, x_scales, "e5m2")
    a = f64(taps)
    Z = V.T @ mxq(f64(kernels), 0, "e4m3")
    y = Z[:, :C] + a[:, 0:1] * Z[:, C:2 * C] + a[:, 1:2] * Z[:, 2 * C:]
    words, scales = planes(y.T)
    return y, words, scales

@@ -1,0 +1,306 @@
+from contextlib import ExitStack
+
+import concourse.mybir as mybir
+from concourse.masks import make_identity
+
+T, K, C = 1536, 1024, 1024
+PARTS = 3
+FLOPS = 2 * T * K * PARTS * C
+
+F32 = mybir.dt.float32
+BF16 = mybir.dt.bfloat16
+U32 = mybir.dt.uint32
+I32 = mybir.dt.int32
+U8 = mybir.dt.uint8
+E4M3X4 = mybir.dt.float8_e4m3fn_x4
+E5M2X4 = mybir.dt.float8_e5m2_x4
+ALU = mybir.AluOpType
+
+P = 128
+PACK = 4
+K_PASS = P * PACK
+PASSES = K // K_PASS
+N = 512
+GROUPS = C // N
+TILES = T // P
+HALF_T = T // 2
+RUN = 4
+Z_BANKS = 6
+GROUPED_BUFS = 3
+ROUNDED_BUFS = 24
+VECTOR_DRAINS = ((0, 2), (0, 4))
+
+
+def note(text):
+    return text
+
+
+def tile_pruned_volterra_equaliser_k2_kernel(tc, x_words, x_scales, taps, kernels, out_0, out_1, out_2):
+    nc = tc.nc
+    with ExitStack() as ctx:
+        keep = ctx.enter_context(tc.tile_pool(name="keep", bufs=1))
+        stage = ctx.enter_context(tc.tile_pool(name="stage", bufs=4))
+        psum = ctx.enter_context(tc.psum_pool(name="psum", bufs=1))
+        ctx.enter_context(tc.manual_schedule())
+
+        raw, grouped, w_codes, w_scales = {}, {}, {}, {}
+        x_codes, acc, rounded, y_codes, y_grouped, banks = {}, {}, {}, {}, {}, {}
+        x_plane = keep.tile([P, PASSES, T], U8, name="x_plane", align_bytes=64)
+        y_planes = [keep.tile([P, T], U8, name="y_plane%d" % g, align_bytes=64) for g in range(GROUPS)]
+        ident = keep.tile([P, P], F32, name="ident")
+        tap_rows = keep.tile([P, 2 * P], BF16, name="tap_rows")
+        tap_cols = keep.tile([P, TILES, 2], F32, name="tap_cols")
+
+        def load_w(key, c0=0, c1=N):
+            g, part, s = key
+            note("w%d%d%d" % key)
+            piece = keep.tile([P, PACK, c1 - c0], BF16, name="raw_%d_%d_%d_%d" % (g, part, s, c0))
+            col = part * C + g * N
+            rows = kernels[s * K_PASS : (s + 1) * K_PASS, col + c0 : col + c1]
+            nc.sync.dma_start(out=piece[:], in_=rows.rearrange("(p j) c -> p j c", j=PACK))
+            raw.setdefault(key, []).append((c0, c1, piece))
+
+        def load_x(s, h):
+            note("x%d%d" % (s, h))
+            x_codes[s, h] = keep.tile([P, HALF_T], U32, name="x_codes_%d_%d" % (s, h), align_bytes=64)
+            words = x_words[s].rearrange("p n t -> p (n t)").bitcast(I32)
+            nc.sync.dma_start(out=x_codes[s, h][:].bitcast(I32), in_=words[:, h * HALF_T : (h + 1) * HALF_T])
+
+        def interleave(key, engine, c0=0, c1=N):
+            note("il%d%d%d" % key)
+            if key not in grouped:
+                if engine == "gpsimd":
+                    grouped[key] = stage.tile([P, N, PACK], BF16, name="grouped_g", align_bytes=64, bufs=1)
+                else:
+                    grouped[key] = stage.tile([P, N, PACK], BF16, name="grouped", align_bytes=64, bufs=GROUPED_BUFS)
+            r0, r1, piece = [r for r in raw[key] if r[0] <= c0 and c1 <= r[1]][0]
+            dst = grouped[key][:, c0:c1, :].rearrange("p (c i) j -> p c j i", i=RUN)
+            src = piece[:, :, c0 - r0 : c1 - r0].rearrange("p j (c i) -> p c j i", i=RUN)
+            if engine == "vector":
+                nc.vector.tensor_copy(out=dst, in_=src)
+            elif engine == "scalar":
+                nc.scalar.copy(out=dst, in_=src)
+            else:
+                nc.gpsimd.tensor_scalar(out=dst, in0=src, scalar1=1.0, scalar2=-0.0, op0=ALU.mult, op1=ALU.add)
+
+        def quantize_w(key, c0=0, c1=N):
+            note("q%d%d%d" % key)
+            if key not in w_codes:
+                w_codes[key] = keep.tile([P, N], U32, name="w_codes_%d_%d_%d" % key, align_bytes=64)
+                w_scales[key] = keep.tile([P, N], U8, name="w_scales_%d_%d_%d" % key, align_bytes=64)
+            nc.vector.quantize_mx(
+                out=w_codes[key][:, c0:c1].bitcast(E4M3X4),
+                scales=w_scales[key][:, c0:c1],
+                in_=grouped[key][:, c0:c1, :].rearrange("p c j -> p (c j)"),
+            )
+
+        def one_pass(g, part, i, s):
+            note("%d%d.%d" % (g, part, i))
+            if s == 0:
+                banks[g, part, i] = psum.tile([P, N], F32, name="z", bufs=Z_BANKS)
+            h, m0 = divmod(i * P, HALF_T)
+            nc.tensor.matmul_mx(
+                out=banks[g, part, i][:],
+                lhsT=x_codes[s, h][:, m0 : m0 + P].bitcast(E5M2X4),
+                lhsT_scale=x_plane[:, s, i * P : (i + 1) * P],
+                rhs=w_codes[g, part, s][:].bitcast(E4M3X4),
+                rhs_scale=w_scales[g, part, s][:],
+                start=(s == 0),
+                stop=(s == PASSES - 1),
+            )
+
+        def drain(g, part, i):
+            note("%d%d.%d" % (g, part, i))
+            z = banks[g, part, i]
+            if part == 0:
+                acc[g, i] = keep.tile([P, N], F32, name="acc_%d_%d" % (g, i))
+                if (g, i) in VECTOR_DRAINS:
+                    nc.vector.tensor_copy(out=acc[g, i][:], in_=z[:])
+                else:
+                    nc.scalar.copy(out=acc[g, i][:], in_=z[:])
+                return
+            if (g, part, i) == (GROUPS - 1, PARTS - 1, TILES - 1):
+                rounded[g, i] = stage.tile([P, 2, P, 2], BF16, name="rounded", bufs=ROUNDED_BUFS)
+                for u in range(2):
+                    nc.vector.scalar_tensor_tensor(
+                        out=rounded[g, i][:, u, :, :],
+                        in0=z[:].rearrange("p (q u e) -> p u q e", u=2, e=2)[:, u, :, :],
+                        scalar=tap_cols[:, i, part - 1 : part],
+                        in1=acc[g, i][:].rearrange("p (q u e) -> p u q e", u=2, e=2)[:, u, :, :],
+                        op0=ALU.mult, op1=ALU.add,
+                    )
+            nc.vector.scalar_tensor_tensor(
+                out=acc[g, i][:], in0=z[:], scalar=tap_cols[:, i, part - 1 : part], in1=acc[g, i][:],
+                op0=ALU.mult, op1=ALU.add,
+            )
+            if part == PARTS - 1:
+                nc.sync.dma_start(out=out_0[i * P : (i + 1) * P, g * N : (g + 1) * N], in_=acc[g, i][:])
+
+        def unit(g, part, i):
+            for s in range(PASSES):
+                one_pass(g, part, i, s)
+            drain(g, part, i)
+
+        def round_y(g, i, engine):
+            note("r%d.%d" % (g, i))
+            rounded[g, i] = stage.tile([P, 2, P, 2], BF16, name="rounded", bufs=ROUNDED_BUFS)
+            src = acc[g, i][:].rearrange("p (q u e) -> p u q e", u=2, e=2)
+            if engine == "vector":
+                nc.vector.tensor_copy(out=rounded[g, i][:], in_=src)
+            elif engine == "scalar":
+                nc.scalar.copy(out=rounded[g, i][:], in_=src)
+            else:
+                nc.gpsimd.tensor_scalar(out=rounded[g, i][:], in0=src, scalar1=1.0, scalar2=-0.0, op0=ALU.mult, op1=ALU.add)
+
+        def turn(g, tiles):
+            note("t%d.%d" % (g, tiles[0]))
+            pairs = [tiles[j : j + 2] for j in range(0, len(tiles), 2)]
+            held = []
+            for pair in pairs:
+                bank = psum.tile([P, 2, 2, P], F32, name="turned", bufs=2)
+                for j, i in enumerate(pair):
+                    words = rounded[g, i][:].rearrange("p u q e -> p (u q e)").bitcast(F32)
+                    for u in range(2):
+                        nc.tensor.transpose(bank[:, j, u, :], words[:, u * P : (u + 1) * P], ident[:])
+                held.append(bank)
+            for pair, bank in zip(pairs, held):
+                quad, j0 = divmod(pair[0], 4)
+                if (g, quad) not in y_grouped:
+                    y_grouped[g, quad] = stage.tile([P, 4 * P, PACK], BF16, name="y_grouped", align_bytes=64, bufs=3)
+                    y_codes[g, quad] = stage.tile([P, 4 * P], U32, name="y_codes", align_bytes=64, bufs=3)
+                words_out = y_grouped[g, quad][:].rearrange("p m t -> p (m t)").bitcast(F32)
+                dst = words_out[:, j0 * 2 * P : (j0 + len(pair)) * 2 * P].rearrange("p (j m u) -> p j m u", u=2, m=P)
+                nc.scalar.copy(out=dst, in_=bank[:, : len(pair), :, :].rearrange("p j u m -> p j m u"))
+
+        def quantize_y(g, tiles):
+            note("qy%d.%d" % (g, tiles[0]))
+            quad, j0 = divmod(tiles[0], 4)
+            m0, w = tiles[0] * P, len(tiles) * P
+            cols = slice(j0 * P, j0 * P + w)
+            codes = y_codes[g, quad]
+            nc.vector.quantize_mx(
+                out=codes[:, cols].bitcast(E4M3X4),
+                scales=y_planes[g][:, m0 : m0 + w],
+                in_=y_grouped[g, quad][:, cols, :].rearrange("p m t -> p (m t)"),
+            )
+            words = out_1[g].rearrange("p m t -> p (m t)").bitcast(I32)
+            nc.sync.dma_start(out=words[:, m0 : m0 + w], in_=codes[:, cols].bitcast(I32))
+
+        def store_scales(g, m0, m1, engines):
+            note("sc%d" % g)
+            for q in range(4):
+                engines[q % len(engines)].dma_start(
+                    out=out_2[g, 4 * q : 4 * q + 4, m0:m1].bitcast(I32),
+                    in_=y_planes[g][32 * q : 32 * q + 4, m0:m1].bitcast(I32),
+                )
+
+        def load_x_scales():
+            note("xs")
+            for q in range(4):
+                nc.sync.dma_start(
+                    out=x_plane[32 * q : 32 * q + 4, :, :].bitcast(I32),
+                    in_=x_scales[:, 4 * q : 4 * q + 4, :].rearrange("s r n -> r s n").bitcast(I32),
+                )
+
+        def load_taps():
+            note("taps")
+            nc.sync.dma_start(out=tap_rows[:TILES, :], in_=taps.rearrange("(i p) a -> i (p a)", p=P))
+
+        def turn_taps():
+            note("taps")
+            bank = psum.tile([P, 2, 2, P], F32, name="turned", bufs=2)
+            nc.tensor.transpose(bank[:, 0, 0, :], tap_rows[:].bitcast(F32), ident[:])
+            nc.scalar.copy(
+                out=tap_cols[:].rearrange("p i a -> p (i a)"),
+                in_=bank[:, 0, 0, :TILES].bitcast(BF16),
+            )
+
+
+        A, B, Cc, D, E, F = (0, 0), (0, 1), (0, 2), (1, 0), (1, 1), (1, 2)
+        nc.vector.memset(x_plane[:].rearrange("p s n -> p (s n)").bitcast(I32), 0)
+        nc.vector.memset(tap_rows[:].bitcast(I32), 0)
+        nc.vector.memset(ident[:], 0.0)
+        make_identity(nc, ident[:], nomemset=True)
+        load_w(A + (0,), 0, 256)
+        load_w(A + (0,), 256, 512)
+        load_x_scales()
+        load_x(0, 0)
+        load_w(A + (1,))
+        load_x(1, 0)
+        load_taps()
+        load_w(B + (0,))
+        load_x(0, 1)
+        load_x(1, 1)
+        load_w(B + (1,))
+        for key in (D, Cc, E, F):
+            for s in range(PASSES):
+                load_w(key + (s,))
+
+        interleave(A + (0,), "vector", 0, 256)
+        interleave(A + (0,), "scalar", 384, 512)
+        interleave(A + (0,), "vector", 256, 384)
+        quantize_w(A + (0,), 0, 256)
+        quantize_w(A + (0,), 256, 512)
+        interleave(A + (1,), "scalar", 320, 512)
+        interleave(A + (1,), "vector", 0, 320)
+        for i in range(Z_BANKS):
+            one_pass(0, 0, i, 0)
+        quantize_w(A + (1,))
+        turn_taps()
+
+        side = {}
+
+        def at(n, fn, *args):
+            side.setdefault(n, []).append((fn, args))
+
+        order = [(0, 0, i) for i in range(TILES)]
+        order += [(0, 1, i) for i in range(9)]
+        for j in range(3):
+            order += [(1, 0, j), (0, 1, 9 + j)]
+        order += [(1, 0, 3), (1, 0, 4), (1, 0, 5)]
+        for j in range(6):
+            order += [(0, 2, 2 * j), (0, 2, 2 * j + 1), (1, 0, 6 + j)]
+        for i in range(TILES):
+            order += [(1, 1, i), (1, 2, i)]
+
+        at(0, interleave, B + (0,), "vector")
+        at(3, quantize_w, B + (0,))
+        at(6, interleave, B + (1,), "vector", 0, 256)
+        at(6, interleave, B + (1,), "vector", 256, 512)
+        at(6, quantize_w, B + (1,), 0, 256)
+        at(6, quantize_w, B + (1,), 256, 512)
+        for part, n_g, n_s, n_q in ((D, 7, (12, 12), 17), (Cc, 18, (18, 18), 25), (E, 26, (26, 31), 34), (F, 35, (34, 37), 43)):
+            at(n_g, interleave, part + (0,), "gpsimd")
+            at(n_s[0], interleave, part + (1,), "scalar", 0, 256)
+            at(n_s[1], interleave, part + (1,), "scalar", 256, 512)
+            at(n_q, quantize_w, part + (1,))
+            at(n_q, quantize_w, part + (0,))
+        for i in range(8):
+            at(44, round_y, 0, i, "gpsimd")
+        for i in range(8, 12):
+            at(38 + i, round_y, 0, i, "scalar")
+        for n, (g, part, i) in enumerate(order):
+            if part == 2 and g == 1 and i < 11:
+                at(n + 1, round_y, g, i, "scalar")
+        for j in range(3):
+            at(52 + 4 * j, turn, 0, list(range(4 * j, 4 * j + 4)))
+            at(55 + 4 * j, quantize_y, 0, list(range(4 * j, 4 * j + 4)))
+        at(64, store_scales, 0, 0, T, [nc.sync])
+        at(64, turn, 1, [0, 1, 2, 3])
+        at(67, quantize_y, 1, [0, 1, 2, 3])
+        at(68, turn, 1, [4, 5, 6, 7])
+        at(72, quantize_y, 1, [4, 5, 6, 7])
+        at(72, turn, 1, [8, 9, 10])
+        at(73, turn, 1, [11])
+        at(73, quantize_y, 1, [8, 9])
+        at(73, quantize_y, 1, [10, 11])
+        at(73, store_scales, 1, 0, T, [nc.sync, nc.scalar])
+
+        for n in range(len(order) + 2):
+            for fn, args in side.get(n, []):
+                fn(*args)
+            if n < Z_BANKS:
+                one_pass(0, 0, n, 1)
+                drain(0, 0, n)
+            elif n < len(order):
+                unit(*order[n])

@@ -23,12 +23,14 @@ PASSES = K // K_PASS
 N = 512
 GROUPS = C // N
 TILES = T // P
-HALF_T = T // 2
+HALF_T = T // 3
 RUN = 4
 Z_BANKS = 6
+AHEAD = 4
 GROUPED_BUFS = 3
 ROUNDED_BUFS = 24
-VECTOR_DRAINS = ((0, 2), (0, 4))
+VECTOR_DRAINS = ((0, 1),)
+SLOT_KEYS = {(0, 1, 1): "x", (0, 2, 0): "x", (1, 1, 1): "y", (1, 2, 0): "y", (1, 0, 0): "y", (1, 1, 0): "y"}
 
 
 def note(text):
@@ -69,8 +71,8 @@ def tile_pruned_volterra_equaliser_k2_kernel(tc, x_words, x_scales, taps, kernel
         def interleave(key, engine, c0=0, c1=N):
             note("il%d%d%d" % key)
             if key not in grouped:
-                if engine == "gpsimd":
-                    grouped[key] = stage.tile([P, N, PACK], BF16, name="grouped_g", align_bytes=64, bufs=1)
+                if key in SLOT_KEYS:
+                    grouped[key] = stage.tile([P, N, PACK], BF16, name="grouped_" + SLOT_KEYS[key], align_bytes=64, bufs=1)
                 else:
                     grouped[key] = stage.tile([P, N, PACK], BF16, name="grouped", align_bytes=64, bufs=GROUPED_BUFS)
             r0, r1, piece = [r for r in raw[key] if r[0] <= c0 and c1 <= r[1]][0]
@@ -81,6 +83,8 @@ def tile_pruned_volterra_equaliser_k2_kernel(tc, x_words, x_scales, taps, kernel
             elif engine == "scalar":
                 nc.scalar.copy(out=dst, in_=src)
             else:
+                dst = grouped[key][:, c0:c1, :]
+                src = piece[:, :, c0 - r0 : c1 - r0].rearrange("p j c -> p c j")
                 nc.gpsimd.tensor_scalar(out=dst, in0=src, scalar1=1.0, scalar2=-0.0, op0=ALU.mult, op1=ALU.add)
 
         def quantize_w(key, c0=0, c1=N):
@@ -129,8 +133,11 @@ def tile_pruned_volterra_equaliser_k2_kernel(tc, x_words, x_scales, taps, kernel
                         in1=acc[g, i][:].rearrange("p (q u e) -> p u q e", u=2, e=2)[:, u, :, :],
                         op0=ALU.mult, op1=ALU.add,
                     )
+            before = acc[g, i]
+            if (g, part, i) == (GROUPS - 1, PARTS - 1, TILES - 1):
+                acc[g, i] = keep.tile([P, N], F32, name="acc_last")
             nc.vector.scalar_tensor_tensor(
-                out=acc[g, i][:], in0=z[:], scalar=tap_cols[:, i, part - 1 : part], in1=acc[g, i][:],
+                out=acc[g, i][:], in0=z[:], scalar=tap_cols[:, i, part - 1 : part], in1=before[:],
                 op0=ALU.mult, op1=ALU.add,
             )
             if part == PARTS - 1:
@@ -204,12 +211,15 @@ def tile_pruned_volterra_equaliser_k2_kernel(tc, x_words, x_scales, taps, kernel
 
         def load_taps():
             note("taps")
-            nc.sync.dma_start(out=tap_rows[:TILES, :], in_=taps.rearrange("(i p) a -> i (p a)", p=P))
+            nc.scalar.dma_start(out=tap_rows[:TILES, :], in_=taps.rearrange("(i p) a -> i (p a)", p=P))
 
         def turn_taps():
             note("taps")
             bank = psum.tile([P, 2, 2, P], F32, name="turned", bufs=2)
             nc.tensor.transpose(bank[:, 0, 0, :], tap_rows[:].bitcast(F32), ident[:])
+            return bank
+
+        def copy_taps(bank):
             nc.scalar.copy(
                 out=tap_cols[:].rearrange("p i a -> p (i a)"),
                 in_=bank[:, 0, 0, :TILES].bitcast(BF16),
@@ -217,81 +227,95 @@ def tile_pruned_volterra_equaliser_k2_kernel(tc, x_words, x_scales, taps, kernel
 
 
         A, B, Cc, D, E, F = (0, 0), (0, 1), (0, 2), (1, 0), (1, 1), (1, 2)
-        nc.vector.memset(x_plane[:].rearrange("p s n -> p (s n)").bitcast(I32), 0)
         nc.vector.memset(tap_rows[:].bitcast(I32), 0)
+        nc.vector.memset(x_plane[:].rearrange("p s n -> p (s n)").bitcast(I32), 0)
         nc.vector.memset(ident[:], 0.0)
         make_identity(nc, ident[:], nomemset=True)
         load_w(A + (0,), 0, 256)
         load_w(A + (0,), 256, 512)
-        load_x_scales()
-        load_x(0, 0)
-        load_w(A + (1,))
-        load_x(1, 0)
         load_taps()
-        load_w(B + (0,))
+        load_x(0, 0)
+        load_x_scales()
+        load_w(A + (1,), 0, 256)
+        load_w(A + (1,), 256, 512)
+        load_x(1, 0)
         load_x(0, 1)
         load_x(1, 1)
+        load_w(B + (0,))
         load_w(B + (1,))
+        load_x(0, 2)
+        load_x(1, 2)
         for key in (D, Cc, E, F):
             for s in range(PASSES):
                 load_w(key + (s,))
 
-        interleave(A + (0,), "vector", 0, 256)
-        interleave(A + (0,), "scalar", 384, 512)
-        interleave(A + (0,), "vector", 256, 384)
-        quantize_w(A + (0,), 0, 256)
-        quantize_w(A + (0,), 256, 512)
-        interleave(A + (1,), "scalar", 320, 512)
-        interleave(A + (1,), "vector", 0, 320)
-        for i in range(Z_BANKS):
-            one_pass(0, 0, i, 0)
-        quantize_w(A + (1,))
-        turn_taps()
+        tap_bank = turn_taps()
+        for s in range(PASSES):
+            interleave(A + (s,), "vector", 0, 256)
+            interleave(A + (s,), "scalar", 384, 512)
+            interleave(A + (s,), "vector", 256, 384)
+            quantize_w(A + (s,), 0, 256)
+            quantize_w(A + (s,), 256, 512)
+            if s == 0:
+                for i in range(AHEAD):
+                    one_pass(0, 0, i, 0)
 
+        copy_taps(tap_bank)
         side = {}
 
         def at(n, fn, *args):
             side.setdefault(n, []).append((fn, args))
 
+        NB = 10
         order = [(0, 0, i) for i in range(TILES)]
-        order += [(0, 1, i) for i in range(9)]
-        for j in range(3):
-            order += [(1, 0, j), (0, 1, 9 + j)]
-        order += [(1, 0, 3), (1, 0, 4), (1, 0, 5)]
+        order += [(0, 1, i) for i in range(NB)]
+        rest = TILES - NB
+        for j in range(rest):
+            order += [(1, 0, i) for i in range(j * 6 // rest, (j + 1) * 6 // rest)] + [(0, 1, NB + j)]
         for j in range(6):
             order += [(0, 2, 2 * j), (0, 2, 2 * j + 1), (1, 0, 6 + j)]
+        order += [(1, 1, 0)]
         for i in range(TILES):
-            order += [(1, 1, i), (1, 2, i)]
+            order += ([(1, 1, i + 1)] if i + 1 < TILES else []) + [(1, 2, i)]
+        pos = {u: n for n, u in enumerate(order)}
 
-        at(0, interleave, B + (0,), "vector")
-        at(3, quantize_w, B + (0,))
-        at(6, interleave, B + (1,), "vector", 0, 256)
-        at(6, interleave, B + (1,), "vector", 256, 512)
-        at(6, quantize_w, B + (1,), 0, 256)
-        at(6, quantize_w, B + (1,), 256, 512)
-        for part, n_g, n_s, n_q in ((D, 7, (12, 12), 17), (Cc, 18, (18, 18), 25), (E, 26, (26, 31), 34), (F, 35, (34, 37), 43)):
-            at(n_g, interleave, part + (0,), "gpsimd")
-            at(n_s[0], interleave, part + (1,), "scalar", 0, 256)
-            at(n_s[1], interleave, part + (1,), "scalar", 256, 512)
-            at(n_q, quantize_w, part + (1,))
-            at(n_q, quantize_w, part + (0,))
-        for i in range(8):
-            at(44, round_y, 0, i, "gpsimd")
-        for i in range(8, 12):
-            at(38 + i, round_y, 0, i, "scalar")
-        for n, (g, part, i) in enumerate(order):
-            if part == 2 and g == 1 and i < 11:
-                at(n + 1, round_y, g, i, "scalar")
-        for j in range(3):
-            at(52 + 4 * j, turn, 0, list(range(4 * j, 4 * j + 4)))
-            at(55 + 4 * j, quantize_y, 0, list(range(4 * j, 4 * j + 4)))
-        at(64, store_scales, 0, 0, T, [nc.sync])
-        at(64, turn, 1, [0, 1, 2, 3])
-        at(67, quantize_y, 1, [0, 1, 2, 3])
-        at(68, turn, 1, [4, 5, 6, 7])
-        at(72, quantize_y, 1, [4, 5, 6, 7])
-        at(72, turn, 1, [8, 9, 10])
-        at(73, turn, 1, [11])
+        at(2, interleave, B + (0,), "vector")
+        at(2, interleave, B + (1,), "vector", 0, 256)
+        at(2, quantize_w, B + (0,))
+        at(2, interleave, B + (1,), "vector", 256, 512)
+        at(2, quantize_w, B + (1,), 0, 256)
+        at(2, quantize_w, B + (1,), 256, 512)
+        at(12, interleave, D + (0,), "vector")
+        at(12, interleave, Cc + (0,), "gpsimd")
+        halves = [(key, 256 * h) for key in (D + (1,), Cc + (1,), F + (1,)) for h in range(2)]
+        slots = [12, 12, 12, 12] + [pos[1, 0, i] + 1 for i in (2,4)]
+        for n, (key, c0) in zip(slots, halves):
+            at(n, interleave, key, "scalar", c0, c0 + 256)
+        qd, qc, qf = pos[1, 0, 0] - 5, pos[0, 2, 0] - 3, pos[1, 1, 0] - 3
+        qe = (qc + qf) // 2 + 1
+        at(qd, quantize_w, D + (1,))
+        at(qd, quantize_w, D + (0,))
+        at(qd, interleave, E + (0,), "gpsimd")
+        at(qc, quantize_w, Cc + (1,))
+        at(qc, quantize_w, Cc + (0,))
+        at(qc, quantize_w, E + (0,))
+        at(qc, interleave, E + (1,), "gpsimd")
+        at(qe, quantize_w, E + (1,))
+        at(qe, interleave, F + (0,), "gpsimd")
+        at(qf, quantize_w, F + (1,))
+        at(qf, quantize_w, F + (0,))
+        for i in range(12):
+            at(max(34 + i, pos[0, 2, i] + 1), round_y, 0, i, "scalar")
+        for i in range(TILES - 1):
+            at(pos[1, 2, i] + 1, round_y, 1, i, "gpsimd" if i < 0 else "scalar")
+        quads = [(g, list(range(4 * j, 4 * j + 4))) for g in range(GROUPS) for j in range(3)][:5]
+        turns = (46,52,56,62,68,72)
+        for j, (g, tiles) in enumerate(quads):
+            at(turns[j], turn, g, tiles)
+            at(turns[j + 1], quantize_y, g, tiles)
+        at(turns[3], store_scales, 0, 0, T, [nc.sync])
+        at(73, turn, 1, [8, 9])
+        at(73, turn, 1, [10, 11])
         at(73, quantize_y, 1, [8, 9])
         at(73, quantize_y, 1, [10, 11])
         at(73, store_scales, 1, 0, T, [nc.sync, nc.scalar])
@@ -299,7 +323,7 @@ def tile_pruned_volterra_equaliser_k2_kernel(tc, x_words, x_scales, taps, kernel
         for n in range(len(order) + 2):
             for fn, args in side.get(n, []):
                 fn(*args)
-            if n < Z_BANKS:
+            if n < AHEAD:
                 one_pass(0, 0, n, 1)
                 drain(0, 0, n)
             elif n < len(order):

@@ -23,30 +23,30 @@ PASSES = K // K_PASS
 N = 512
 GROUPS = C // N
 TILES = T // P
-HALF_T = T // 3
+QUAD = 4
+QUAD_T = QUAD * P
+HALF = N // 2
+BANKS = 8
 RUN = 4
-Z_BANKS = 6
 AHEAD = 4
-GROUPED_BUFS = 3
-ROUNDED_BUFS = 24
-VECTOR_DRAINS = ((0, 1),)
-SLOT_KEYS = {(0, 1, 1): "x", (0, 2, 0): "x", (1, 1, 1): "y", (1, 2, 0): "y", (1, 0, 0): "y", (1, 1, 0): "y"}
-
-
-def note(text):
-    return text
+SCALAR_SHARE = 128
+LONE_UNITS = 10
+LEAD_NEXT_GROUP = 5
+LEAD = 3
+FIRST_ROUND = 34
+SETTLE = 4
 
 
 def tile_pruned_volterra_equaliser_k2_kernel(tc, x_words, x_scales, taps, kernels, out_0, out_1, out_2):
     nc = tc.nc
     with ExitStack() as ctx:
         keep = ctx.enter_context(tc.tile_pool(name="keep", bufs=1))
-        stage = ctx.enter_context(tc.tile_pool(name="stage", bufs=4))
-        psum = ctx.enter_context(tc.psum_pool(name="psum", bufs=1))
+        stage = ctx.enter_context(tc.tile_pool(name="stage", bufs=3))
+        psum = ctx.enter_context(tc.psum_pool(name="psum", bufs=BANKS))
         ctx.enter_context(tc.manual_schedule())
 
         raw, grouped, w_codes, w_scales = {}, {}, {}, {}
-        x_codes, acc, rounded, y_codes, y_grouped, banks = {}, {}, {}, {}, {}, {}
+        x_codes, z_banks, acc, rounded, y_grouped, y_codes = {}, {}, {}, {}, {}, {}
         x_plane = keep.tile([P, PASSES, T], U8, name="x_plane", align_bytes=64)
         y_planes = [keep.tile([P, T], U8, name="y_plane%d" % g, align_bytes=64) for g in range(GROUPS)]
         ident = keep.tile([P, P], F32, name="ident")
@@ -55,40 +55,37 @@ def tile_pruned_volterra_equaliser_k2_kernel(tc, x_words, x_scales, taps, kernel
 
         def load_w(key, c0=0, c1=N):
             g, part, s = key
-            note("w%d%d%d" % key)
             piece = keep.tile([P, PACK, c1 - c0], BF16, name="raw_%d_%d_%d_%d" % (g, part, s, c0))
             col = part * C + g * N
             rows = kernels[s * K_PASS : (s + 1) * K_PASS, col + c0 : col + c1]
             nc.sync.dma_start(out=piece[:], in_=rows.rearrange("(p j) c -> p j c", j=PACK))
             raw.setdefault(key, []).append((c0, c1, piece))
 
-        def load_x(s, h):
-            note("x%d%d" % (s, h))
-            x_codes[s, h] = keep.tile([P, HALF_T], U32, name="x_codes_%d_%d" % (s, h), align_bytes=64)
+        def load_x(s, quad):
+            x_codes[s, quad] = keep.tile([P, QUAD_T], U32, name="x_codes_%d_%d" % (s, quad), align_bytes=64)
             words = x_words[s].rearrange("p n t -> p (n t)").bitcast(I32)
-            nc.sync.dma_start(out=x_codes[s, h][:].bitcast(I32), in_=words[:, h * HALF_T : (h + 1) * HALF_T])
+            nc.sync.dma_start(out=x_codes[s, quad][:].bitcast(I32), in_=words[:, quad * QUAD_T : (quad + 1) * QUAD_T])
 
-        def interleave(key, engine, c0=0, c1=N):
-            note("il%d%d%d" % key)
+        def load_x_scales(m0, m1):
+            rows = x_scales.rearrange("s (q r) n -> r q s n", r=4)
+            for r in range(4):
+                nc.sync.dma_start(out=x_plane[r:P:32, :, m0:m1].bitcast(I32), in_=rows[r][:, :, m0:m1].bitcast(I32))
+
+        def interleave(key, engine, c0=0, c1=N, tag="grouped"):
             if key not in grouped:
-                if key in SLOT_KEYS:
-                    grouped[key] = stage.tile([P, N, PACK], BF16, name="grouped_" + SLOT_KEYS[key], align_bytes=64, bufs=1)
-                else:
-                    grouped[key] = stage.tile([P, N, PACK], BF16, name="grouped", align_bytes=64, bufs=GROUPED_BUFS)
+                grouped[key] = stage.tile([P, N, PACK], BF16, name=tag, align_bytes=64, bufs=3 if tag == "grouped" else 1)
             r0, r1, piece = [r for r in raw[key] if r[0] <= c0 and c1 <= r[1]][0]
-            dst = grouped[key][:, c0:c1, :].rearrange("p (c i) j -> p c j i", i=RUN)
-            src = piece[:, :, c0 - r0 : c1 - r0].rearrange("p j (c i) -> p c j i", i=RUN)
-            if engine == "vector":
-                nc.vector.tensor_copy(out=dst, in_=src)
-            elif engine == "scalar":
-                nc.scalar.copy(out=dst, in_=src)
-            else:
-                dst = grouped[key][:, c0:c1, :]
-                src = piece[:, :, c0 - r0 : c1 - r0].rearrange("p j c -> p c j")
-                nc.gpsimd.tensor_scalar(out=dst, in0=src, scalar1=1.0, scalar2=-0.0, op0=ALU.mult, op1=ALU.add)
+            dst = grouped[key][:, c0:c1, :]
+            src = piece[:, :, c0 - r0 : c1 - r0]
+            if engine is nc.gpsimd:
+                nc.gpsimd.tensor_scalar(
+                    out=dst, in0=src.rearrange("p j c -> p c j"), scalar1=1.0, scalar2=-0.0, op0=ALU.mult, op1=ALU.add
+                )
+                return
+            copy = nc.vector.tensor_copy if engine is nc.vector else nc.scalar.copy
+            copy(out=dst.rearrange("p (c i) j -> p c j i", i=RUN), in_=src.rearrange("p j (c i) -> p c j i", i=RUN))
 
         def quantize_w(key, c0=0, c1=N):
-            note("q%d%d%d" % key)
             if key not in w_codes:
                 w_codes[key] = keep.tile([P, N], U32, name="w_codes_%d_%d_%d" % key, align_bytes=64)
                 w_scales[key] = keep.tile([P, N], U8, name="w_scales_%d_%d_%d" % key, align_bytes=64)
@@ -99,13 +96,12 @@ def tile_pruned_volterra_equaliser_k2_kernel(tc, x_words, x_scales, taps, kernel
             )
 
         def one_pass(g, part, i, s):
-            note("%d%d.%d" % (g, part, i))
             if s == 0:
-                banks[g, part, i] = psum.tile([P, N], F32, name="z", bufs=Z_BANKS)
-            h, m0 = divmod(i * P, HALF_T)
+                z_banks[g, part, i] = psum.tile([P, N], F32, name="bank")
+            quad, j = divmod(i, QUAD)
             nc.tensor.matmul_mx(
-                out=banks[g, part, i][:],
-                lhsT=x_codes[s, h][:, m0 : m0 + P].bitcast(E5M2X4),
+                out=z_banks[g, part, i][:],
+                lhsT=x_codes[s, quad][:, j * P : (j + 1) * P].bitcast(E5M2X4),
                 lhsT_scale=x_plane[:, s, i * P : (i + 1) * P],
                 rhs=w_codes[g, part, s][:].bitcast(E4M3X4),
                 rhs_scale=w_scales[g, part, s][:],
@@ -113,218 +109,187 @@ def tile_pruned_volterra_equaliser_k2_kernel(tc, x_words, x_scales, taps, kernel
                 stop=(s == PASSES - 1),
             )
 
+        def word_order(ap):
+            return ap.rearrange("p (q u e) -> p u q e", u=2, e=2)
+
+        def new_rounded(g, i):
+            rounded[g, i] = keep.tile([P, 2, P, 2], BF16, name="rounded_%d_%d" % (g, i))
+            return rounded[g, i]
+
+        def add_part(out, z, part, i, before):
+            nc.vector.scalar_tensor_tensor(
+                out=out, in0=z, scalar=tap_cols[:, i, part - 1 : part], in1=before, op0=ALU.mult, op1=ALU.add
+            )
+
+        def store_y(g, i):
+            nc.sync.dma_start(out=out_0[i * P : (i + 1) * P, g * N : (g + 1) * N], in_=acc[g, i][:])
+
         def drain(g, part, i):
-            note("%d%d.%d" % (g, part, i))
-            z = banks[g, part, i]
+            z = z_banks[g, part, i]
             if part == 0:
                 acc[g, i] = keep.tile([P, N], F32, name="acc_%d_%d" % (g, i))
-                if (g, i) in VECTOR_DRAINS:
-                    nc.vector.tensor_copy(out=acc[g, i][:], in_=z[:])
-                else:
-                    nc.scalar.copy(out=acc[g, i][:], in_=z[:])
+                copy = nc.vector.tensor_copy if (g, i) == (0, 1) else nc.scalar.copy
+                copy(out=acc[g, i][:], in_=z[:])
                 return
-            if (g, part, i) == (GROUPS - 1, PARTS - 1, TILES - 1):
-                rounded[g, i] = stage.tile([P, 2, P, 2], BF16, name="rounded", bufs=ROUNDED_BUFS)
-                for u in range(2):
-                    nc.vector.scalar_tensor_tensor(
-                        out=rounded[g, i][:, u, :, :],
-                        in0=z[:].rearrange("p (q u e) -> p u q e", u=2, e=2)[:, u, :, :],
-                        scalar=tap_cols[:, i, part - 1 : part],
-                        in1=acc[g, i][:].rearrange("p (q u e) -> p u q e", u=2, e=2)[:, u, :, :],
-                        op0=ALU.mult, op1=ALU.add,
-                    )
-            before = acc[g, i]
-            if (g, part, i) == (GROUPS - 1, PARTS - 1, TILES - 1):
-                acc[g, i] = keep.tile([P, N], F32, name="acc_last")
-            nc.vector.scalar_tensor_tensor(
-                out=acc[g, i][:], in0=z[:], scalar=tap_cols[:, i, part - 1 : part], in1=before[:],
-                op0=ALU.mult, op1=ALU.add,
-            )
+            add_part(acc[g, i][:], z[:], part, i, acc[g, i][:])
             if part == PARTS - 1:
-                nc.sync.dma_start(out=out_0[i * P : (i + 1) * P, g * N : (g + 1) * N], in_=acc[g, i][:])
-
-        def unit(g, part, i):
-            for s in range(PASSES):
-                one_pass(g, part, i, s)
-            drain(g, part, i)
+                store_y(g, i)
 
         def round_y(g, i, engine):
-            note("r%d.%d" % (g, i))
-            rounded[g, i] = stage.tile([P, 2, P, 2], BF16, name="rounded", bufs=ROUNDED_BUFS)
-            src = acc[g, i][:].rearrange("p (q u e) -> p u q e", u=2, e=2)
-            if engine == "vector":
-                nc.vector.tensor_copy(out=rounded[g, i][:], in_=src)
-            elif engine == "scalar":
-                nc.scalar.copy(out=rounded[g, i][:], in_=src)
-            else:
-                nc.gpsimd.tensor_scalar(out=rounded[g, i][:], in0=src, scalar1=1.0, scalar2=-0.0, op0=ALU.mult, op1=ALU.add)
+            copy = nc.vector.tensor_copy if engine is nc.vector else nc.scalar.copy
+            copy(out=new_rounded(g, i)[:], in_=word_order(acc[g, i][:]))
 
-        def turn(g, tiles):
-            note("t%d.%d" % (g, tiles[0]))
-            pairs = [tiles[j : j + 2] for j in range(0, len(tiles), 2)]
+        def turn(pairs):
             held = []
-            for pair in pairs:
-                bank = psum.tile([P, 2, 2, P], F32, name="turned", bufs=2)
-                for j, i in enumerate(pair):
-                    words = rounded[g, i][:].rearrange("p u q e -> p (u q e)").bitcast(F32)
+            for g, first in pairs:
+                bank = psum.tile([P, 2, 2, P], F32, name="bank")
+                for j in range(2):
+                    words = rounded[g, first + j][:].rearrange("p u q e -> p (u q e)").bitcast(F32)
                     for u in range(2):
                         nc.tensor.transpose(bank[:, j, u, :], words[:, u * P : (u + 1) * P], ident[:])
                 held.append(bank)
-            for pair, bank in zip(pairs, held):
-                quad, j0 = divmod(pair[0], 4)
-                if (g, quad) not in y_grouped:
-                    y_grouped[g, quad] = stage.tile([P, 4 * P, PACK], BF16, name="y_grouped", align_bytes=64, bufs=3)
-                    y_codes[g, quad] = stage.tile([P, 4 * P], U32, name="y_codes", align_bytes=64, bufs=3)
-                words_out = y_grouped[g, quad][:].rearrange("p m t -> p (m t)").bitcast(F32)
-                dst = words_out[:, j0 * 2 * P : (j0 + len(pair)) * 2 * P].rearrange("p (j m u) -> p j m u", u=2, m=P)
-                nc.scalar.copy(out=dst, in_=bank[:, : len(pair), :, :].rearrange("p j u m -> p j m u"))
+            for (g, first), bank in zip(pairs, held):
+                quad, j = divmod(first, QUAD)
+                if j == 0:
+                    y_grouped[g, quad] = stage.tile([P, QUAD_T, PACK], BF16, name="y_grouped", align_bytes=64)
+                    y_codes[g, quad] = stage.tile([P, QUAD_T], U32, name="y_codes", align_bytes=64)
+                words = y_grouped[g, quad][:, j * P : (j + 2) * P, :].rearrange("p m t -> p (m t)").bitcast(F32)
+                nc.scalar.copy(
+                    out=words.rearrange("p (j m u) -> p j m u", u=2, m=P), in_=bank[:].rearrange("p j u m -> p j m u")
+                )
 
-        def quantize_y(g, tiles):
-            note("qy%d.%d" % (g, tiles[0]))
-            quad, j0 = divmod(tiles[0], 4)
-            m0, w = tiles[0] * P, len(tiles) * P
-            cols = slice(j0 * P, j0 * P + w)
-            codes = y_codes[g, quad]
+        def quantize_y(g, first, count):
+            quad, j = divmod(first, QUAD)
+            cols = slice(j * P, (j + count) * P)
+            instants = slice(first * P, (first + count) * P)
             nc.vector.quantize_mx(
-                out=codes[:, cols].bitcast(E4M3X4),
-                scales=y_planes[g][:, m0 : m0 + w],
+                out=y_codes[g, quad][:, cols].bitcast(E4M3X4),
+                scales=y_planes[g][:, instants],
                 in_=y_grouped[g, quad][:, cols, :].rearrange("p m t -> p (m t)"),
             )
             words = out_1[g].rearrange("p m t -> p (m t)").bitcast(I32)
-            nc.sync.dma_start(out=words[:, m0 : m0 + w], in_=codes[:, cols].bitcast(I32))
+            nc.sync.dma_start(out=words[:, instants], in_=y_codes[g, quad][:, cols].bitcast(I32))
 
-        def store_scales(g, m0, m1, engines):
-            note("sc%d" % g)
-            for q in range(4):
-                engines[q % len(engines)].dma_start(
-                    out=out_2[g, 4 * q : 4 * q + 4, m0:m1].bitcast(I32),
-                    in_=y_planes[g][32 * q : 32 * q + 4, m0:m1].bitcast(I32),
-                )
+        def store_scales(g, queues):
+            rows = out_2[g].rearrange("(q r) m -> r q m", r=4)
+            for r in range(4):
+                queues[r % len(queues)].dma_start(out=rows[r].bitcast(I32), in_=y_planes[g][r:P:32, :].bitcast(I32))
 
-        def load_x_scales():
-            note("xs")
-            for q in range(4):
-                nc.sync.dma_start(
-                    out=x_plane[32 * q : 32 * q + 4, :, :].bitcast(I32),
-                    in_=x_scales[:, 4 * q : 4 * q + 4, :].rearrange("s r n -> r s n").bitcast(I32),
-                )
-
-        def load_taps():
-            note("taps")
-            nc.scalar.dma_start(out=tap_rows[:TILES, :], in_=taps.rearrange("(i p) a -> i (p a)", p=P))
-
-        def turn_taps():
-            note("taps")
-            bank = psum.tile([P, 2, 2, P], F32, name="turned", bufs=2)
-            nc.tensor.transpose(bank[:, 0, 0, :], tap_rows[:].bitcast(F32), ident[:])
-            return bank
-
-        def copy_taps(bank):
-            nc.scalar.copy(
-                out=tap_cols[:].rearrange("p i a -> p (i a)"),
-                in_=bank[:, 0, 0, :TILES].bitcast(BF16),
-            )
-
-
-        A, B, Cc, D, E, F = (0, 0), (0, 1), (0, 2), (1, 0), (1, 1), (1, 2)
         nc.vector.memset(tap_rows[:].bitcast(I32), 0)
         nc.vector.memset(x_plane[:].rearrange("p s n -> p (s n)").bitcast(I32), 0)
         nc.vector.memset(ident[:], 0.0)
         make_identity(nc, ident[:], nomemset=True)
-        load_w(A + (0,), 0, 256)
-        load_w(A + (0,), 256, 512)
-        load_taps()
-        load_x(0, 0)
-        load_x_scales()
-        load_w(A + (1,), 0, 256)
-        load_w(A + (1,), 256, 512)
-        load_x(1, 0)
-        load_x(0, 1)
-        load_x(1, 1)
-        load_w(B + (0,))
-        load_w(B + (1,))
-        load_x(0, 2)
-        load_x(1, 2)
-        for key in (D, Cc, E, F):
-            for s in range(PASSES):
-                load_w(key + (s,))
 
-        tap_bank = turn_taps()
+        for c0 in (0, HALF):
+            load_w((0, 0, 0), c0, c0 + HALF)
+        nc.scalar.dma_start(out=tap_rows[:TILES, :], in_=taps.rearrange("(i p) a -> i (p a)", p=P))
+        load_x(0, 0)
+        load_x_scales(0, T)
+        for c0 in (0, HALF):
+            load_w((0, 0, 1), c0, c0 + HALF)
+        load_x(1, 0)
         for s in range(PASSES):
-            interleave(A + (s,), "vector", 0, 256)
-            interleave(A + (s,), "scalar", 384, 512)
-            interleave(A + (s,), "vector", 256, 384)
-            quantize_w(A + (s,), 0, 256)
-            quantize_w(A + (s,), 256, 512)
+            load_x(s, 1)
+        for s in range(PASSES):
+            load_w((0, 1, s))
+        for s in range(PASSES):
+            load_x(s, 2)
+        for g, part in ((1, 0), (0, 2), (1, 1), (1, 2)):
+            for s in range(PASSES):
+                load_w((g, part, s))
+
+        tap_bank = psum.tile([P, P], F32, name="bank")
+        nc.tensor.transpose(tap_bank[:], tap_rows[:].bitcast(F32), ident[:])
+        for s in range(PASSES):
+            key = (0, 0, s)
+            interleave(key, nc.vector, 0, HALF)
+            interleave(key, nc.scalar, N - SCALAR_SHARE, N)
+            interleave(key, nc.vector, HALF, N - SCALAR_SHARE)
+            for c0 in (0, HALF):
+                quantize_w(key, c0, c0 + HALF)
             if s == 0:
                 for i in range(AHEAD):
                     one_pass(0, 0, i, 0)
+        nc.scalar.copy(out=tap_cols[:].rearrange("p i a -> p (i a)"), in_=tap_bank[:, :TILES].bitcast(BF16))
 
-        copy_taps(tap_bank)
-        side = {}
-
-        def at(n, fn, *args):
-            side.setdefault(n, []).append((fn, args))
-
-        NB = 10
-        order = [(0, 0, i) for i in range(TILES)]
-        order += [(0, 1, i) for i in range(NB)]
-        rest = TILES - NB
+        order = [(0, 0, i) for i in range(TILES)] + [(0, 1, i) for i in range(LONE_UNITS)]
+        rest, half_tiles = TILES - LONE_UNITS, TILES // 2
         for j in range(rest):
-            order += [(1, 0, i) for i in range(j * 6 // rest, (j + 1) * 6 // rest)] + [(0, 1, NB + j)]
-        for j in range(6):
-            order += [(0, 2, 2 * j), (0, 2, 2 * j + 1), (1, 0, 6 + j)]
-        order += [(1, 1, 0)]
-        for i in range(TILES):
-            order += ([(1, 1, i + 1)] if i + 1 < TILES else []) + [(1, 2, i)]
+            order.extend((1, 0, i) for i in range(j * half_tiles // rest, (j + 1) * half_tiles // rest))
+            order.append((0, 1, LONE_UNITS + j))
+        for j in range(half_tiles):
+            order.extend([(0, 2, 2 * j), (0, 2, 2 * j + 1), (1, 0, half_tiles + j)])
+        order.append((1, 1, 0))
+        for i in range(TILES - 1):
+            order.extend([(1, 1, i + 1), (1, 2, i)])
+        order.append((1, 2, TILES - 1))
         pos = {u: n for n, u in enumerate(order)}
 
-        at(2, interleave, B + (0,), "vector")
-        at(2, interleave, B + (1,), "vector", 0, 256)
-        at(2, quantize_w, B + (0,))
-        at(2, interleave, B + (1,), "vector", 256, 512)
-        at(2, quantize_w, B + (1,), 0, 256)
-        at(2, quantize_w, B + (1,), 256, 512)
-        at(12, interleave, D + (0,), "vector")
-        at(12, interleave, Cc + (0,), "gpsimd")
-        halves = [(key, 256 * h) for key in (D + (1,), Cc + (1,), F + (1,)) for h in range(2)]
-        slots = [12, 12, 12, 12] + [pos[1, 0, i] + 1 for i in (2,4)]
-        for n, (key, c0) in zip(slots, halves):
-            at(n, interleave, key, "scalar", c0, c0 + 256)
-        qd, qc, qf = pos[1, 0, 0] - 5, pos[0, 2, 0] - 3, pos[1, 1, 0] - 3
-        qe = (qc + qf) // 2 + 1
-        at(qd, quantize_w, D + (1,))
-        at(qd, quantize_w, D + (0,))
-        at(qd, interleave, E + (0,), "gpsimd")
-        at(qc, quantize_w, Cc + (1,))
-        at(qc, quantize_w, Cc + (0,))
-        at(qc, quantize_w, E + (0,))
-        at(qc, interleave, E + (1,), "gpsimd")
-        at(qe, quantize_w, E + (1,))
-        at(qe, interleave, F + (0,), "gpsimd")
-        at(qf, quantize_w, F + (1,))
-        at(qf, quantize_w, F + (0,))
-        for i in range(12):
-            at(max(34 + i, pos[0, 2, i] + 1), round_y, 0, i, "scalar")
-        for i in range(TILES - 1):
-            at(pos[1, 2, i] + 1, round_y, 1, i, "gpsimd" if i < 0 else "scalar")
-        quads = [(g, list(range(4 * j, 4 * j + 4))) for g in range(GROUPS) for j in range(3)][:5]
-        turns = (46,52,56,62,68,72)
-        for j, (g, tiles) in enumerate(quads):
-            at(turns[j], turn, g, tiles)
-            at(turns[j + 1], quantize_y, g, tiles)
-        at(turns[3], store_scales, 0, 0, T, [nc.sync])
-        at(73, turn, 1, [8, 9])
-        at(73, turn, 1, [10, 11])
-        at(73, quantize_y, 1, [8, 9])
-        at(73, quantize_y, 1, [10, 11])
-        at(73, store_scales, 1, 0, T, [nc.sync, nc.scalar])
+        before = {}
 
-        for n in range(len(order) + 2):
-            for fn, args in side.get(n, []):
+        def at(n, fn, *args):
+            before.setdefault(n, []).append((fn, args))
+
+        at(2, interleave, (0, 1, 0), nc.vector)
+        at(2, interleave, (0, 1, 1), nc.vector, 0, HALF, "grouped_a")
+        at(2, quantize_w, (0, 1, 0))
+        at(2, interleave, (0, 1, 1), nc.vector, HALF, N)
+        at(2, quantize_w, (0, 1, 1), 0, HALF)
+        at(2, quantize_w, (0, 1, 1), HALF, N)
+        at(TILES, interleave, (1, 0, 0), nc.vector, 0, N, "grouped_b")
+        at(TILES, interleave, (1, 0, 1), nc.gpsimd, 0, N, "grouped_a")
+        for key in ((0, 2, 0), (0, 2, 1)):
+            for c0 in (0, HALF):
+                at(TILES, interleave, key, nc.scalar, c0, c0 + HALF)
+        for h in range(2):
+            at(pos[1, 0, 2 * h + 2] + 1, interleave, (1, 2, 1), nc.scalar, h * HALF, (h + 1) * HALF)
+        first, second, last = pos[1, 0, 0] - LEAD_NEXT_GROUP, pos[0, 2, 0] - LEAD, pos[1, 1, 0] - LEAD
+        third = (second + last + 1) // 2
+        for n, keys, following in (
+            (first, ((1, 0, 1), (1, 0, 0)), (1, 1, 0)),
+            (second, ((0, 2, 0), (0, 2, 1), (1, 1, 0)), (1, 1, 1)),
+            (third, ((1, 1, 1),), (1, 2, 0)),
+        ):
+            for key in keys:
+                at(n, quantize_w, key)
+            at(n, interleave, following, nc.gpsimd, 0, N, "grouped_b")
+        for key in ((1, 2, 1), (1, 2, 0)):
+            at(last, quantize_w, key)
+        for i in range(TILES):
+            at(max(FIRST_ROUND + i, pos[0, 2, i] + 1), round_y, 0, i, nc.scalar)
+        for i in range(TILES - 2):
+            at(pos[1, 2, i] + 1, round_y, 1, i, nc.scalar)
+        runs = (pos[1, 1, 0], pos[1, 2, QUAD + 1], pos[1, 2, 2 * QUAD + 1])
+        at(runs[0], turn, [(0, 0), (0, 2), (0, 4), (0, 6)])
+        at(runs[0] + SETTLE, quantize_y, 0, 0, QUAD)
+        at(runs[1], turn, [(0, 8), (0, 10), (1, 0), (1, 2)])
+        at(runs[1], quantize_y, 0, QUAD, QUAD)
+        at(runs[1] + SETTLE, quantize_y, 0, 2 * QUAD, QUAD)
+        at(runs[1] + SETTLE, store_scales, 0, [nc.sync])
+        at(runs[2], turn, [(1, 4), (1, 6)])
+        at(runs[2], quantize_y, 1, 0, QUAD)
+
+        for n, (g, part, i) in enumerate(order[:-1]):
+            for fn, args in before.get(n, []):
                 fn(*args)
-            if n < AHEAD:
-                one_pass(0, 0, n, 1)
-                drain(0, 0, n)
-            elif n < len(order):
-                unit(*order[n])
+            for s in range(1 if n < AHEAD else 0, PASSES):
+                one_pass(g, part, i, s)
+            drain(g, part, i)
+
+        g, part, i = order[-1]
+        for s in range(PASSES):
+            one_pass(g, part, i, s)
+        z, partial = z_banks[g, part, i], acc[g, i]
+        last_rounded = new_rounded(g, i)
+        for u in range(2):
+            add_part(last_rounded[:, u, :, :], word_order(z[:])[:, u, :, :], part, i, word_order(partial[:])[:, u, :, :])
+        round_y(g, i - 1, nc.scalar)
+        acc[g, i] = keep.tile([P, N], F32, name="acc_last")
+        add_part(acc[g, i][:], z[:], part, i, partial[:])
+        store_y(g, i)
+        turn([(1, 8)])
+        turn([(1, 10)])
+        quantize_y(1, 4, 4)
+        quantize_y(1, 8, 2)
+        quantize_y(1, 10, 2)
+        store_scales(1, [nc.sync, nc.scalar])

@@ -33,8 +33,7 @@ SCALAR_SHARE = 128
 LONE_UNITS = 10
 LEAD_NEXT_GROUP = 5
 LEAD = 3
-FIRST_ROUND = 34
-SETTLE = 4
+RUN_GAP = 6
 
 
 def tile_pruned_volterra_equaliser_k2_kernel(tc, x_words, x_scales, taps, kernels, out_0, out_1, out_2):
@@ -135,9 +134,11 @@ def tile_pruned_volterra_equaliser_k2_kernel(tc, x_words, x_scales, taps, kernel
             if part == PARTS - 1:
                 store_y(g, i)
 
-        def round_y(g, i, engine):
-            copy = nc.vector.tensor_copy if engine is nc.vector else nc.scalar.copy
-            copy(out=new_rounded(g, i)[:], in_=word_order(acc[g, i][:]))
+        def round_y(g, i):
+            nc.scalar.copy(
+                out=new_rounded(g, i)[:].rearrange("p u (a b) e -> p a u b e", b=RUN),
+                in_=word_order(acc[g, i][:]).rearrange("p u (a b) e -> p a u b e", b=RUN),
+            )
 
         def turn(pairs):
             held = []
@@ -255,19 +256,20 @@ def tile_pruned_volterra_equaliser_k2_kernel(tc, x_words, x_scales, taps, kernel
             at(n, interleave, following, nc.gpsimd, 0, N, "grouped_b")
         for key in ((1, 2, 1), (1, 2, 0)):
             at(last, quantize_w, key)
+        first_round = pos[1, 0, half_tiles] + 1
         for i in range(TILES):
-            at(max(FIRST_ROUND + i, pos[0, 2, i] + 1), round_y, 0, i, nc.scalar)
+            at(max(first_round + i, pos[0, 2, i] + 1), round_y, 0, i)
         for i in range(TILES - 2):
-            at(pos[1, 2, i] + 1, round_y, 1, i, nc.scalar)
-        runs = (pos[1, 1, 0], pos[1, 2, QUAD + 1], pos[1, 2, 2 * QUAD + 1])
-        at(runs[0], turn, [(0, 0), (0, 2), (0, 4), (0, 6)])
-        at(runs[0] + SETTLE, quantize_y, 0, 0, QUAD)
-        at(runs[1], turn, [(0, 8), (0, 10), (1, 0), (1, 2)])
-        at(runs[1], quantize_y, 0, QUAD, QUAD)
-        at(runs[1] + SETTLE, quantize_y, 0, 2 * QUAD, QUAD)
-        at(runs[1] + SETTLE, store_scales, 0, [nc.sync])
-        at(runs[2], turn, [(1, 4), (1, 6)])
-        at(runs[2], quantize_y, 1, 0, QUAD)
+            at(pos[1, 2, i] + 1, round_y, 1, i)
+        quads = [(g, first) for g in range(GROUPS) for first in range(0, TILES, QUAD)][:-1]
+        last_run = pos[1, 2, quads[-1][1] + QUAD + 1]
+        for j, (g, first) in enumerate(quads):
+            n = last_run - RUN_GAP * (len(quads) - 1 - j)
+            at(n, turn, [(g, first), (g, first + 2)])
+            if j > 0:
+                at(n, quantize_y, *quads[j - 1], QUAD)
+            if (g, first) == (1, 0):
+                at(n, store_scales, 0, [nc.sync])
 
         for n, (g, part, i) in enumerate(order[:-1]):
             for fn, args in before.get(n, []):
@@ -283,13 +285,14 @@ def tile_pruned_volterra_equaliser_k2_kernel(tc, x_words, x_scales, taps, kernel
         last_rounded = new_rounded(g, i)
         for u in range(2):
             add_part(last_rounded[:, u, :, :], word_order(z[:])[:, u, :, :], part, i, word_order(partial[:])[:, u, :, :])
-        round_y(g, i - 1, nc.scalar)
+        round_y(g, i - 1)
         acc[g, i] = keep.tile([P, N], F32, name="acc_last")
         add_part(acc[g, i][:], z[:], part, i, partial[:])
         store_y(g, i)
-        turn([(1, 8)])
-        turn([(1, 10)])
-        quantize_y(1, 4, 4)
-        quantize_y(1, 8, 2)
-        quantize_y(1, 10, 2)
-        store_scales(1, [nc.sync, nc.scalar])
+        last_pairs = (TILES - QUAD, TILES - 2)
+        for first in last_pairs:
+            turn([(g, first)])
+        quantize_y(*quads[-1], QUAD)
+        for first in last_pairs:
+            quantize_y(g, first, 2)
+        store_scales(g, [nc.sync, nc.scalar])

from contextlib import ExitStack

import concourse.mybir as mybir
from concourse.masks import make_identity

T, K, C = 1536, 1024, 1024
PARTS = 3
FLOPS = 2 * T * K * PARTS * C

F32 = mybir.dt.float32
BF16 = mybir.dt.bfloat16
U32 = mybir.dt.uint32
I32 = mybir.dt.int32
U8 = mybir.dt.uint8
E4M3X4 = mybir.dt.float8_e4m3fn_x4
E5M2X4 = mybir.dt.float8_e5m2_x4
ALU = mybir.AluOpType

P = 128
PACK = 4
K_PASS = P * PACK
PASSES = K // K_PASS
N = 512
GROUPS = C // N
TILES = T // P
QUAD = 4
QUAD_T = QUAD * P
HALF = N // 2
BANKS = 8
RUN = 4
AHEAD = 4
SCALAR_SHARE = 128
LONE_UNITS = 10
LEAD_NEXT_GROUP = 5
LEAD = 3
RUN_GAP = 6


def tile_pruned_volterra_equaliser_k2_kernel(tc, x_words, x_scales, taps, kernels, out_0, out_1, out_2):
    nc = tc.nc
    with ExitStack() as ctx:
        keep = ctx.enter_context(tc.tile_pool(name="keep", bufs=1))
        stage = ctx.enter_context(tc.tile_pool(name="stage", bufs=3))
        psum = ctx.enter_context(tc.psum_pool(name="psum", bufs=BANKS))
        ctx.enter_context(tc.manual_schedule())

        raw, grouped, w_codes, w_scales = {}, {}, {}, {}
        x_codes, z_banks, acc, rounded, y_grouped, y_codes = {}, {}, {}, {}, {}, {}
        x_plane = keep.tile([P, PASSES, T], U8, name="x_plane", align_bytes=64)
        y_planes = [keep.tile([P, T], U8, name="y_plane%d" % g, align_bytes=64) for g in range(GROUPS)]
        ident = keep.tile([P, P], F32, name="ident")
        tap_rows = keep.tile([P, 2 * P], BF16, name="tap_rows")
        tap_cols = keep.tile([P, TILES, 2], F32, name="tap_cols")

        def load_w(key, c0=0, c1=N):
            g, part, s = key
            piece = keep.tile([P, PACK, c1 - c0], BF16, name="raw_%d_%d_%d_%d" % (g, part, s, c0))
            col = part * C + g * N
            rows = kernels[s * K_PASS : (s + 1) * K_PASS, col + c0 : col + c1]
            nc.sync.dma_start(out=piece[:], in_=rows.rearrange("(p j) c -> p j c", j=PACK))
            raw.setdefault(key, []).append((c0, c1, piece))

        def load_x(s, quad):
            x_codes[s, quad] = keep.tile([P, QUAD_T], U32, name="x_codes_%d_%d" % (s, quad), align_bytes=64)
            words = x_words[s].rearrange("p n t -> p (n t)").bitcast(I32)
            nc.sync.dma_start(out=x_codes[s, quad][:].bitcast(I32), in_=words[:, quad * QUAD_T : (quad + 1) * QUAD_T])

        def load_x_scales(m0, m1):
            rows = x_scales.rearrange("s (q r) n -> r q s n", r=4)
            for r in range(4):
                nc.sync.dma_start(out=x_plane[r:P:32, :, m0:m1].bitcast(I32), in_=rows[r][:, :, m0:m1].bitcast(I32))

        def interleave(key, engine, c0=0, c1=N, tag="grouped"):
            if key not in grouped:
                grouped[key] = stage.tile([P, N, PACK], BF16, name=tag, align_bytes=64, bufs=3 if tag == "grouped" else 1)
            r0, r1, piece = [r for r in raw[key] if r[0] <= c0 and c1 <= r[1]][0]
            dst = grouped[key][:, c0:c1, :]
            src = piece[:, :, c0 - r0 : c1 - r0]
            if engine is nc.gpsimd:
                nc.gpsimd.tensor_scalar(
                    out=dst, in0=src.rearrange("p j c -> p c j"), scalar1=1.0, scalar2=-0.0, op0=ALU.mult, op1=ALU.add
                )
                return
            copy = nc.vector.tensor_copy if engine is nc.vector else nc.scalar.copy
            copy(out=dst.rearrange("p (c i) j -> p c j i", i=RUN), in_=src.rearrange("p j (c i) -> p c j i", i=RUN))

        def quantize_w(key, c0=0, c1=N):
            if key not in w_codes:
                w_codes[key] = keep.tile([P, N], U32, name="w_codes_%d_%d_%d" % key, align_bytes=64)
                w_scales[key] = keep.tile([P, N], U8, name="w_scales_%d_%d_%d" % key, align_bytes=64)
            nc.vector.quantize_mx(
                out=w_codes[key][:, c0:c1].bitcast(E4M3X4),
                scales=w_scales[key][:, c0:c1],
                in_=grouped[key][:, c0:c1, :].rearrange("p c j -> p (c j)"),
            )

        def one_pass(g, part, i, s):
            if s == 0:
                z_banks[g, part, i] = psum.tile([P, N], F32, name="bank")
            quad, j = divmod(i, QUAD)
            nc.tensor.matmul_mx(
                out=z_banks[g, part, i][:],
                lhsT=x_codes[s, quad][:, j * P : (j + 1) * P].bitcast(E5M2X4),
                lhsT_scale=x_plane[:, s, i * P : (i + 1) * P],
                rhs=w_codes[g, part, s][:].bitcast(E4M3X4),
                rhs_scale=w_scales[g, part, s][:],
                start=(s == 0),
                stop=(s == PASSES - 1),
            )

        def word_order(ap):
            return ap.rearrange("p (q u e) -> p u q e", u=2, e=2)

        def new_rounded(g, i):
            rounded[g, i] = keep.tile([P, 2, P, 2], BF16, name="rounded_%d_%d" % (g, i))
            return rounded[g, i]

        def add_part(out, z, part, i, before):
            nc.vector.scalar_tensor_tensor(
                out=out, in0=z, scalar=tap_cols[:, i, part - 1 : part], in1=before, op0=ALU.mult, op1=ALU.add
            )

        def store_y(g, i):
            nc.sync.dma_start(out=out_0[i * P : (i + 1) * P, g * N : (g + 1) * N], in_=acc[g, i][:])

        def drain(g, part, i):
            z = z_banks[g, part, i]
            if part == 0:
                acc[g, i] = keep.tile([P, N], F32, name="acc_%d_%d" % (g, i))
                copy = nc.vector.tensor_copy if (g, i) == (0, 1) else nc.scalar.copy
                copy(out=acc[g, i][:], in_=z[:])
                return
            add_part(acc[g, i][:], z[:], part, i, acc[g, i][:])
            if part == PARTS - 1:
                store_y(g, i)

        def round_y(g, i):
            nc.scalar.copy(
                out=new_rounded(g, i)[:].rearrange("p u (a b) e -> p a u b e", b=RUN),
                in_=word_order(acc[g, i][:]).rearrange("p u (a b) e -> p a u b e", b=RUN),
            )

        def turn(pairs):
            held = []
            for g, first in pairs:
                bank = psum.tile([P, 2, 2, P], F32, name="bank")
                for j in range(2):
                    words = rounded[g, first + j][:].rearrange("p u q e -> p (u q e)").bitcast(F32)
                    for u in range(2):
                        nc.tensor.transpose(bank[:, j, u, :], words[:, u * P : (u + 1) * P], ident[:])
                held.append(bank)
            for (g, first), bank in zip(pairs, held):
                quad, j = divmod(first, QUAD)
                if j == 0:
                    y_grouped[g, quad] = stage.tile([P, QUAD_T, PACK], BF16, name="y_grouped", align_bytes=64)
                    y_codes[g, quad] = stage.tile([P, QUAD_T], U32, name="y_codes", align_bytes=64)
                words = y_grouped[g, quad][:, j * P : (j + 2) * P, :].rearrange("p m t -> p (m t)").bitcast(F32)
                nc.scalar.copy(
                    out=words.rearrange("p (j m u) -> p j m u", u=2, m=P), in_=bank[:].rearrange("p j u m -> p j m u")
                )

        def quantize_y(g, first, count):
            quad, j = divmod(first, QUAD)
            cols = slice(j * P, (j + count) * P)
            instants = slice(first * P, (first + count) * P)
            nc.vector.quantize_mx(
                out=y_codes[g, quad][:, cols].bitcast(E4M3X4),
                scales=y_planes[g][:, instants],
                in_=y_grouped[g, quad][:, cols, :].rearrange("p m t -> p (m t)"),
            )
            words = out_1[g].rearrange("p m t -> p (m t)").bitcast(I32)
            nc.sync.dma_start(out=words[:, instants], in_=y_codes[g, quad][:, cols].bitcast(I32))

        def store_scales(g, queues):
            rows = out_2[g].rearrange("(q r) m -> r q m", r=4)
            for r in range(4):
                queues[r % len(queues)].dma_start(out=rows[r].bitcast(I32), in_=y_planes[g][r:P:32, :].bitcast(I32))

        nc.vector.memset(tap_rows[:].bitcast(I32), 0)
        nc.vector.memset(x_plane[:].rearrange("p s n -> p (s n)").bitcast(I32), 0)
        nc.vector.memset(ident[:], 0.0)
        make_identity(nc, ident[:], nomemset=True)

        for c0 in (0, HALF):
            load_w((0, 0, 0), c0, c0 + HALF)
        nc.scalar.dma_start(out=tap_rows[:TILES, :], in_=taps.rearrange("(i p) a -> i (p a)", p=P))
        load_x(0, 0)
        load_x_scales(0, T)
        for c0 in (0, HALF):
            load_w((0, 0, 1), c0, c0 + HALF)
        load_x(1, 0)
        for s in range(PASSES):
            load_x(s, 1)
        for s in range(PASSES):
            load_w((0, 1, s))
        for s in range(PASSES):
            load_x(s, 2)
        for g, part in ((1, 0), (0, 2), (1, 1), (1, 2)):
            for s in range(PASSES):
                load_w((g, part, s))

        tap_bank = psum.tile([P, P], F32, name="bank")
        nc.tensor.transpose(tap_bank[:], tap_rows[:].bitcast(F32), ident[:])
        for s in range(PASSES):
            key = (0, 0, s)
            interleave(key, nc.vector, 0, HALF)
            interleave(key, nc.scalar, N - SCALAR_SHARE, N)
            interleave(key, nc.vector, HALF, N - SCALAR_SHARE)
            for c0 in (0, HALF):
                quantize_w(key, c0, c0 + HALF)
            if s == 0:
                for i in range(AHEAD):
                    one_pass(0, 0, i, 0)
        nc.scalar.copy(out=tap_cols[:].rearrange("p i a -> p (i a)"), in_=tap_bank[:, :TILES].bitcast(BF16))

        order = [(0, 0, i) for i in range(TILES)] + [(0, 1, i) for i in range(LONE_UNITS)]
        rest, half_tiles = TILES - LONE_UNITS, TILES // 2
        for j in range(rest):
            order.extend((1, 0, i) for i in range(j * half_tiles // rest, (j + 1) * half_tiles // rest))
            order.append((0, 1, LONE_UNITS + j))
        for j in range(half_tiles):
            order.extend([(0, 2, 2 * j), (0, 2, 2 * j + 1), (1, 0, half_tiles + j)])
        order.append((1, 1, 0))
        for i in range(TILES - 1):
            order.extend([(1, 1, i + 1), (1, 2, i)])
        order.append((1, 2, TILES - 1))
        pos = {u: n for n, u in enumerate(order)}

        before = {}

        def at(n, fn, *args):
            before.setdefault(n, []).append((fn, args))

        at(2, interleave, (0, 1, 0), nc.vector)
        at(2, interleave, (0, 1, 1), nc.vector, 0, HALF, "grouped_a")
        at(2, quantize_w, (0, 1, 0))
        at(2, interleave, (0, 1, 1), nc.vector, HALF, N)
        at(2, quantize_w, (0, 1, 1), 0, HALF)
        at(2, quantize_w, (0, 1, 1), HALF, N)
        at(TILES, interleave, (1, 0, 0), nc.vector, 0, N, "grouped_b")
        at(TILES, interleave, (1, 0, 1), nc.gpsimd, 0, N, "grouped_a")
        for key in ((0, 2, 0), (0, 2, 1)):
            for c0 in (0, HALF):
                at(TILES, interleave, key, nc.scalar, c0, c0 + HALF)
        for h in range(2):
            at(pos[1, 0, 2 * h + 2] + 1, interleave, (1, 2, 1), nc.scalar, h * HALF, (h + 1) * HALF)
        first, second, last = pos[1, 0, 0] - LEAD_NEXT_GROUP, pos[0, 2, 0] - LEAD, pos[1, 1, 0] - LEAD
        third = (second + last + 1) // 2
        for n, keys, following in (
            (first, ((1, 0, 1), (1, 0, 0)), (1, 1, 0)),
            (second, ((0, 2, 0), (0, 2, 1), (1, 1, 0)), (1, 1, 1)),
            (third, ((1, 1, 1),), (1, 2, 0)),
        ):
            for key in keys:
                at(n, quantize_w, key)
            at(n, interleave, following, nc.gpsimd, 0, N, "grouped_b")
        for key in ((1, 2, 1), (1, 2, 0)):
            at(last, quantize_w, key)
        first_round = pos[1, 0, half_tiles] + 1
        for i in range(TILES):
            at(max(first_round + i, pos[0, 2, i] + 1), round_y, 0, i)
        for i in range(TILES - 2):
            at(pos[1, 2, i] + 1, round_y, 1, i)
        quads = [(g, first) for g in range(GROUPS) for first in range(0, TILES, QUAD)][:-1]
        last_run = pos[1, 2, quads[-1][1] + QUAD + 1]
        for j, (g, first) in enumerate(quads):
            n = last_run - RUN_GAP * (len(quads) - 1 - j)
            at(n, turn, [(g, first), (g, first + 2)])
            if j > 0:
                at(n, quantize_y, *quads[j - 1], QUAD)
            if (g, first) == (1, 0):
                at(n, store_scales, 0, [nc.sync])

        for n, (g, part, i) in enumerate(order[:-1]):
            for fn, args in before.get(n, []):
                fn(*args)
            for s in range(1 if n < AHEAD else 0, PASSES):
                one_pass(g, part, i, s)
            drain(g, part, i)

        g, part, i = order[-1]
        for s in range(PASSES):
            one_pass(g, part, i, s)
        z, partial = z_banks[g, part, i], acc[g, i]
        last_rounded = new_rounded(g, i)
        for u in range(2):
            add_part(last_rounded[:, u, :, :], word_order(z[:])[:, u, :, :], part, i, word_order(partial[:])[:, u, :, :])
        round_y(g, i - 1)
        acc[g, i] = keep.tile([P, N], F32, name="acc_last")
        add_part(acc[g, i][:], z[:], part, i, partial[:])
        store_y(g, i)
        last_pairs = (TILES - QUAD, TILES - 2)
        for first in last_pairs:
            turn([(g, first)])
        quantize_y(*quads[-1], QUAD)
        for first in last_pairs:
            quantize_y(g, first, 2)
        store_scales(g, [nc.sync, nc.scalar])
